import numpy as np
import ml_dtypes


def mxq(x, axis, fmt="e4m3"):
    dtype, down = {"e4m3": (ml_dtypes.float8_e4m3fn, 7), "e5m2": (ml_dtypes.float8_e5m2, 14)}[fmt]
    v = np.moveaxis(np.asarray(x, np.float32).astype(ml_dtypes.bfloat16).astype(np.float64), axis, -1)
    blocks = v.reshape(v.shape[:-1] + (-1, 32))
    amax = np.abs(blocks).max(-1, keepdims=True)
    byte = np.maximum(np.where(amax > 0, np.frexp(amax)[1] - 1 + 127, 0) - down, 1)
    scale = np.exp2(byte - 127.0)
    codes = (blocks / scale).astype(np.float32).astype(dtype).astype(np.float64)
    return np.moveaxis((codes * scale).reshape(v.shape), -1, axis)


WIDE = False


def mx_kscale(k):
    if not WIDE:
        return np.ones(k)
    levels = np.array([10, -10, 5, -5, 0])
    if k % 512:
        return np.exp2(np.random.permutation(np.resize(levels, k // 32))).repeat(32)
    a = np.empty((k // 512, 16))
    for p in range(k // 512):
        a[p, :8] = np.random.permutation(np.resize(levels, 8))
        for g in range(8):
            far = levels[np.abs(levels - a[p, g]) >= 10]
            a[p, g + 8] = far[np.random.randint(len(far))]
    return np.exp2(a.ravel()).repeat(32)


def f64(x):
    return np.asarray(x).astype(np.float64)


def striped(idx):
    return np.tile(idx.reshape(-1, 16).T, (8, 1)).astype(np.uint16)


def unstriped(offs):
    return offs[:16].T.reshape(-1).astype(np.int64)


def striped8(idx):
    return np.concatenate([x.reshape(-1, 16).T for x in idx]).astype(np.uint16)


def runs(offs, k):
    lists = np.stack([offs[16 * r : 16 * r + 16].T.reshape(-1) for r in range(8)]).astype(np.int64)
    return lists[np.arange(k) % 512 // 64]


def pack_weight(w):
    k, n = w.shape
    w = f64(np.asarray(w, np.float32).astype(ml_dtypes.bfloat16)).reshape(k // 32, 32, n)
    amax = np.abs(w).max(1)
    byte = np.clip(np.where(amax > 0, np.frexp(amax)[1] - 1 + 127 - 7, 1), 1, 254)
    scaled = (w * np.exp2(127.0 - byte)[:, None, :]).reshape(k, n).astype(np.float32)
    words = np.ascontiguousarray(scaled.reshape(k // 512, 128, 4, n).transpose(0, 1, 3, 2)).astype(ml_dtypes.float8_e4m3fn).view(np.uint8)
    return words, np.ascontiguousarray(byte.astype(np.uint8).reshape(k // 512, 16, n))


def unpack_weight(words, scales):
    g, p, n, _ = words.shape
    vals = np.ascontiguousarray(words).view(ml_dtypes.float8_e4m3fn).astype(np.float64) * np.repeat(np.exp2(scales.astype(np.float64) - 127.0), 8, axis=1)[..., None]
    return vals.transpose(0, 1, 3, 2).reshape(g * 512, n)

def planes(y):
    n, m = y.shape
    v = y.astype(np.float32).astype(ml_dtypes.bfloat16).astype(np.float64).reshape(n // 32, 32, m)
    top = np.abs(v).max(1)
    byte = np.clip(np.where(top > 0, np.frexp(top)[1] - 1 + 127 - 7, 1), 1, 254)
    codes = (v * np.exp2(127.0 - byte)[:, None, :]).reshape(n, m).astype(np.float32).astype(ml_dtypes.float8_e4m3fn).view(np.uint8)
    words = codes.reshape(n // 512, 128, 4, m).transpose(0, 1, 3, 2)
    return np.ascontiguousarray(words), np.ascontiguousarray(byte.astype(np.uint8).reshape(n // 512, 16, m))


K, T, S, G, H, C = 512, 1024, 512, 2048, 512, 512


def setup_inputs():
    n = np.random.standard_normal
    s = mx_kscale(K)[:, None]
    packed_xT = pack_weight(n((K, T)) * s)
    packed_dT = pack_weight(n((K, G)) / s)
    return {
        "x_words": packed_xT[0],
        "x_scales": packed_xT[1],
        "d_words": packed_dT[0],
        "d_scales": packed_dT[1],
        "gs": (np.random.uniform(0.5, 1.5, (K, 1)) / s).astype(np.float32),
        "offs": striped(np.random.permutation(T)[:S]),
        "k1": striped8(np.random.randint(0, G, (8, H))),
        "n1": striped8(np.stack([np.random.permutation(S) for _ in range(8)])),
        "n2": striped8(np.stack([np.random.permutation(S) for _ in range(8)])),
        "cand": striped(np.random.permutation(T)[:C]),
        "n3": striped8(np.stack([np.random.permutation(S) for _ in range(8)])),
        "n4": striped8(np.stack([np.random.permutation(S) for _ in range(8)])),
    }


def reference(x_words, x_scales, d_words, d_scales, gs, offs, k1, n1, n2, cand, n3, n4):
    x_cand = unpack_weight(x_words, x_scales)[:, unstriped(cand)]
    d_k1 = unpack_weight(d_words, d_scales)[np.arange(K)[:, None], runs(k1, K)]
    xq = unpack_weight(x_words, x_scales)[:, unstriped(offs)]
    h = 0.0625 * (d_k1.T @ xq)
    z = f64(gs) * ((h[np.arange(H)[:, None], runs(n1, H)]) / (np.abs(h) + np.abs(h[np.arange(H)[:, None], runs(n2, H)]) + 0.5))
    s = 0.0625 * ((x_cand.T @ mxq(z, 0, "e4m3")))
    out_0 = s[np.arange(C)[:, None], runs(n3, C)] - (s[np.arange(C)[:, None], runs(n4, C)])
    return (out_0,) + planes(out_0)

@@ -1,0 +1,205 @@
+from contextlib import ExitStack
+
+import concourse.mybir as mybir
+
+F32 = mybir.dt.float32
+BF16 = mybir.dt.bfloat16
+I32 = mybir.dt.int32
+U32 = mybir.dt.uint32
+U16 = mybir.dt.uint16
+U8 = mybir.dt.uint8
+FP8X4 = mybir.dt.float8_e4m3fn_x4
+ACT = mybir.ActivationFunctionType
+ALU = mybir.AluOpType
+
+P = 128
+PACK = 4
+N = 512
+T = 1024
+G = 2048
+PER_COL = 16
+FLOPS = 2 * 2 * 512 * 512 * 512
+
+HALVES = [(0, 256), (256, 512)]
+Z_CHUNKS = [(0, 256), (256, 384), (384, 512)]
+OUT_CHUNKS = [(0, 256), (256, 384), (384, 512)]
+
+
+def cols(lst, lo, hi):
+    return lst[:, lo // PER_COL : hi // PER_COL]
+
+
+def weave(engine_copy, dst, src):
+    engine_copy(
+        out=dst.rearrange("p (c i) t -> p c t i", i=4),
+        in_=src.rearrange("p t (c i) -> p c t i", i=4),
+    )
+
+
+def tile_picked_pqcnorm2gap_none_po_kernel(tc, x_words, x_scales, d_words, d_scales, gs, offs, k1, n1, n2, cand, n3, n4, out_0, out_1, out_2):
+    nc = tc.nc
+    with ExitStack() as ctx:
+        keep = ctx.enter_context(tc.tile_pool(name="keep", bufs=1))
+        stage = ctx.enter_context(tc.tile_pool(name="stage", bufs=1))
+        psum = ctx.enter_context(tc.psum_pool(name="psum", bufs=1))
+
+        def sb(name, shape, dtype):
+            return keep.tile(shape, dtype, name=name, align_bytes=64)
+
+        def load_list(name, src):
+            lst = keep.tile([P, N // PER_COL], U16, name=name)
+            nc.sync.dma_start(lst[:], src)
+            return lst
+
+        warm = sb("warm", [P, 1], F32)
+        warm_out = sb("warm_out", [P, 1], F32)
+        nc.vector.memset(warm[:], 1.0)
+        nc.scalar.activation(warm_out[:], warm[:], ACT.Abs_reciprocal_sqrt)
+
+        xs = sb("xs", [P, T], U8)
+        d_plane = sb("d_plane", [P, N], U8)
+        nc.vector.memset(d_plane[:].bitcast(I32), 0)
+
+        k1_l = load_list("k1_l", k1)
+        ds = sb("ds", [P, G], U8)
+        nc.sync.dma_start(ds[:].bitcast(I32), d_scales[0].bitcast(I32).unsqueeze(1).to_broadcast([16, 8, G // 4]))
+        offs_l = load_list("offs_l", offs)
+        for q in range(4):
+            nc.sync.dma_start(xs[32 * q : 32 * q + 32, :].bitcast(I32), x_scales[0, 4 * q : 4 * q + 4, :].bitcast(I32).unsqueeze(0).to_broadcast([8, 4, T // 4]))
+        dw = sb("dw", [P, G], U32)
+        nc.sync.dma_start(dw[:].bitcast(I32), d_words[0].rearrange("p n t -> p (n t)").bitcast(I32))
+        n2_l = load_list("n2_l", n2)
+        gain = sb("gain", [P, PACK], F32)
+        nc.sync.dma_start(gain[:], gs.rearrange("(p t) o -> p (t o)", t=PACK))
+        n1_l = load_list("n1_l", n1)
+        xw = sb("xw", [P, T], U32)
+        nc.sync.dma_start(xw[:].bitcast(I32), x_words[0].rearrange("p n t -> p (n t)").bitcast(I32))
+        cand_l = load_list("cand_l", cand)
+        n4_l = load_list("n4_l", n4)
+        n3_l = load_list("n3_l", n3)
+
+        def gather(name, table, lst, dtype, offset=None):
+            if offset is None:
+                got = sb(name, [P, N], dtype)
+            else:
+                got = stage.tile([P, N], dtype, name=name, align_bytes=64, offset=offset)
+            nc.vector.tensor_copy(got[:], table[:].indirect(lst[:]))
+            return got
+
+        def deal(name, got, dtype):
+            dealt = sb(name, [P, N], dtype)
+            nc.vector.tensor_copy(dealt[:].rearrange("p (t m) -> p t m", t=PACK), got[:].rearrange("p (m t) -> p t m", t=PACK))
+            return dealt
+
+        ds_dealt = deal("ds_dealt", gather("ds_got", ds, k1_l, U8), U8)
+        for i in range(4):
+            queue = nc.sync if i % 2 == 0 else nc.scalar
+            queue.dma_start(d_plane[i:P:32, :].bitcast(I32), ds_dealt[8 * i : P : 32, :].bitcast(I32))
+        xq_s = gather("xq_s", xs, offs_l, U8)
+        dw_dealt = deal("dw_dealt", gather("dw_got", dw, k1_l, U32, 0), U32)
+        xq_w = gather("xq_w", xw, offs_l, U32)
+
+        h_ps = []
+        for t in range(PACK):
+            bank = psum.tile([P, N], F32, name="bank%d" % t)
+            m = slice(t * P, (t + 1) * P)
+            nc.tensor.matmul_mx(bank[:], lhsT=dw_dealt[:, m].bitcast(FP8X4), lhsT_scale=d_plane[:, m],
+                                rhs=xq_w[:].bitcast(FP8X4), rhs_scale=xq_s[:], start=True, stop=True)
+            h_ps.append(bank)
+
+        xc_w_got = gather("xc_w_got", xw, cand_l, U32, N)
+        xc_s_got = gather("xc_s_got", xs, cand_l, U8, 0)
+        xc_w = deal("xc_w", xc_w_got, U32)
+        xc_s = deal("xc_s", xc_s_got, U8)
+
+        z_f = [sb("z_f%d" % c, [P, PACK, hi - lo], F32) for c, (lo, hi) in enumerate(Z_CHUNKS)]
+        size, size2, num, den, inv = [], [], [], [], []
+        for t in range(PACK):
+            size.append(sb("size%d" % t, [P, N], F32))
+            size2.append(sb("size2_%d" % t, [P, N], F32))
+            num.append(sb("num%d" % t, [P, N], F32))
+            den.append(sb("den%d" % t, [P, N], F32))
+            inv.append(sb("inv%d" % t, [P, N], F32))
+
+        for t in range(PACK):
+            nc.scalar.activation(size[t][:], h_ps[t][:], ACT.Abs, scale=0.0625)
+            if t == 0:
+                nc.scalar.activation(size2[t][:], h_ps[t][:], ACT.Abs, scale=0.0625)
+            else:
+                nc.sync.dma_start(size2[t][:], size[t][:])
+        for t in range(PACK):
+            nc.scalar.activation(num[t][:], h_ps[t][:], ACT.Copy, scale=gain[:, t : t + 1])
+
+        def denominator(t):
+            for lo, hi in HALVES:
+                nc.vector.tensor_tensor(den[t][:, lo:hi], size[t][:].indirect(cols(n2_l, lo, hi)), size2[t][:, lo:hi], ALU.add)
+            root = keep.tile([P, N], F32, name="root%d" % t)
+            nc.scalar.activation(root[:], den[t][:], ACT.Abs_reciprocal_sqrt, bias=0.5)
+            nc.scalar.activation(inv[t][:], root[:], ACT.Square, scale=0.25)
+
+        def quotient(t, c):
+            lo, hi = Z_CHUNKS[c]
+            nc.vector.tensor_tensor(z_f[c][:, t, :], num[t][:].indirect(cols(n1_l, lo, hi)), inv[t][:, lo:hi], ALU.mult)
+
+        score = [sb("score%d" % t, [P, N], F32) for t in range(PACK)]
+        z_b = [sb("z_b%d" % c, [P, hi - lo, PACK], BF16) for c, (lo, hi) in enumerate(Z_CHUNKS)]
+        s_ps = {}
+
+        def multiply(c):
+            lo, hi = Z_CHUNKS[c]
+            w = hi - lo
+            z_w = sb("z_w%d" % c, [P, w], U32)
+            z_s = sb("z_s%d" % c, [P, w], U8)
+            nc.vector.quantize_mx(out=z_w[:].bitcast(FP8X4), scales=z_s[:], in_=z_b[c][:].rearrange("p n t -> p (n t)"))
+            half = lo // 256
+            for t in range(PACK):
+                if (half, t) not in s_ps:
+                    s_ps[(half, t)] = psum.tile([P, N], F32, name="bank%d" % ((PACK * (half + 1) + t) % 8))
+                bank = s_ps[(half, t)]
+                m = slice(t * P, (t + 1) * P)
+                nc.tensor.matmul_mx(bank[:, lo % 256 : lo % 256 + w], lhsT=xc_w[:, m].bitcast(FP8X4), lhsT_scale=xc_s[:, m],
+                                    rhs=z_w[:].bitcast(FP8X4), rhs_scale=z_s[:], start=True, stop=True)
+                if hi % 256 == 0:
+                    nc.scalar.activation(score[t][:, hi - 256 : hi], bank[:, :256], ACT.Copy, scale=0.0625)
+
+        denominator(0)
+        denominator(1)
+        quotient(0, 0)
+        denominator(2)
+        denominator(3)
+        for t in range(1, PACK):
+            quotient(t, 0)
+        weave(nc.scalar.copy, z_b[0][:], z_f[0][:])
+        for t in range(PACK):
+            quotient(t, 1)
+        weave(nc.scalar.copy, z_b[1][:], z_f[1][:])
+        multiply(0)
+        for t in range(PACK):
+            quotient(t, 2)
+        multiply(1)
+        weave(nc.vector.tensor_copy, z_b[2][:], z_f[2][:])
+        multiply(2)
+
+        out_rows = out_0.rearrange("(p t) j -> p t j", t=PACK)
+        out_words = out_1[0].rearrange("p n t -> p (n t)").bitcast(I32)
+        o_s = sb("o_s", [P, N], U8)
+        minus = [sb("minus%d" % t, [P, N], F32) for t in range(PACK)]
+        for c, (lo, hi) in enumerate(OUT_CHUNKS):
+            w = hi - lo
+            last = c == len(OUT_CHUNKS) - 1
+            o_f = sb("o_f%d" % c, [P, PACK, w], F32)
+            for pair in (0, 2):
+                if lo % 256 == 0:
+                    for t in (pair, pair + 1):
+                        nc.vector.tensor_copy(minus[t][:, lo : lo + 256], score[t][:].indirect(cols(n4_l, lo, lo + 256)))
+                for t in (pair, pair + 1):
+                    nc.vector.tensor_tensor(o_f[:, t, :], score[t][:].indirect(cols(n3_l, lo, hi)), minus[t][:, lo:hi], ALU.subtract)
+            nc.sync.dma_start(out_rows[:, :, lo:hi], o_f[:])
+            o_b = sb("o_b%d" % c, [P, w, PACK], BF16)
+            weave(nc.vector.tensor_copy if last else nc.scalar.copy, o_b[:], o_f[:])
+            o_w = sb("o_w%d" % c, [P, w], U32)
+            nc.vector.quantize_mx(out=o_w[:].bitcast(FP8X4), scales=o_s[:, lo:hi], in_=o_b[:].rearrange("p n t -> p (n t)"))
+            nc.sync.dma_start(out_words[:, lo:hi], o_w[:].bitcast(I32))
+        for q in range(4):
+            queue = nc.scalar if q % 4 != 3 else nc.sync
+            queue.dma_start(out_2[0, 4 * q : 4 * q + 4, :].bitcast(I32), o_s[32 * q : 32 * q + 4, :].bitcast(I32))

@@ -60,9 +60,9 @@ def tile_picked_pqcnorm2gap_none_po_kernel(tc, x_words, x_scales, d_words, d_sca
         d_plane = sb("d_plane", [P, N], U8)
         nc.vector.memset(d_plane[:].bitcast(I32), 0)
 
-        k1_l = load_list("k1_l", k1)
         ds = sb("ds", [P, G], U8)
         nc.sync.dma_start(ds[:].bitcast(I32), d_scales[0].bitcast(I32).unsqueeze(1).to_broadcast([16, 8, G // 4]))
+        k1_l = load_list("k1_l", k1)
         offs_l = load_list("offs_l", offs)
         for q in range(4):
             nc.sync.dma_start(xs[32 * q : 32 * q + 32, :].bitcast(I32), x_scales[0, 4 * q : 4 * q + 4, :].bitcast(I32).unsqueeze(0).to_broadcast([8, 4, T // 4]))
@@ -74,9 +74,6 @@ def tile_picked_pqcnorm2gap_none_po_kernel(tc, x_words, x_scales, d_words, d_sca
         n1_l = load_list("n1_l", n1)
         xw = sb("xw", [P, T], U32)
         nc.sync.dma_start(xw[:].bitcast(I32), x_words[0].rearrange("p n t -> p (n t)").bitcast(I32))
-        cand_l = load_list("cand_l", cand)
-        n4_l = load_list("n4_l", n4)
-        n3_l = load_list("n3_l", n3)
 
         def gather(name, table, lst, dtype, offset=None):
             if offset is None:
@@ -88,13 +85,20 @@ def tile_picked_pqcnorm2gap_none_po_kernel(tc, x_words, x_scales, d_words, d_sca
 
         def deal(name, got, dtype):
             dealt = sb(name, [P, N], dtype)
-            nc.vector.tensor_copy(dealt[:].rearrange("p (t m) -> p t m", t=PACK), got[:].rearrange("p (m t) -> p t m", t=PACK))
+            line = 4 if dtype == U32 else 16
+            nc.vector.tensor_copy(
+                dealt[:].rearrange("p (t c i) -> p c t i", t=PACK, i=line),
+                got[:].rearrange("p (c i t) -> p c t i", t=PACK, i=line),
+            )
             return dealt
 
         ds_dealt = deal("ds_dealt", gather("ds_got", ds, k1_l, U8), U8)
         for i in range(4):
             queue = nc.sync if i % 2 == 0 else nc.scalar
             queue.dma_start(d_plane[i:P:32, :].bitcast(I32), ds_dealt[8 * i : P : 32, :].bitcast(I32))
+        cand_l = load_list("cand_l", cand)
+        n4_l = load_list("n4_l", n4)
+        n3_l = load_list("n3_l", n3)
         xq_s = gather("xq_s", xs, offs_l, U8)
         dw_dealt = deal("dw_dealt", gather("dw_got", dw, k1_l, U32, 0), U32)
         xq_w = gather("xq_w", xw, offs_l, U32)
@@ -112,38 +116,49 @@ def tile_picked_pqcnorm2gap_none_po_kernel(tc, x_words, x_scales, d_words, d_sca
         xc_w = deal("xc_w", xc_w_got, U32)
         xc_s = deal("xc_s", xc_s_got, U8)
 
-        z_f = [sb("z_f%d" % c, [P, PACK, hi - lo], F32) for c, (lo, hi) in enumerate(Z_CHUNKS)]
-        size, size2, num, den, inv = [], [], [], [], []
+
+        size, size2, num, den = [], [], [], []
         for t in range(PACK):
             size.append(sb("size%d" % t, [P, N], F32))
-            size2.append(sb("size2_%d" % t, [P, N], F32))
+            if t == 3:
+                size2.append(stage.tile([P, N], F32, name="size2_3", align_bytes=64, offset=4096))
+            else:
+                size2.append(sb("size2_%d" % t, [P, N], F32))
             num.append(sb("num%d" % t, [P, N], F32))
             den.append(sb("den%d" % t, [P, N], F32))
-            inv.append(sb("inv%d" % t, [P, N], F32))
 
         for t in range(PACK):
             nc.scalar.activation(size[t][:], h_ps[t][:], ACT.Abs, scale=0.0625)
-            if t == 0:
+            if t == 2:
                 nc.scalar.activation(size2[t][:], h_ps[t][:], ACT.Abs, scale=0.0625)
             else:
                 nc.sync.dma_start(size2[t][:], size[t][:])
-        for t in range(PACK):
+
+        inv = {}
+
+        def numerator(t):
             nc.scalar.activation(num[t][:], h_ps[t][:], ACT.Copy, scale=gain[:, t : t + 1])
 
         def denominator(t):
             for lo, hi in HALVES:
                 nc.vector.tensor_tensor(den[t][:, lo:hi], size[t][:].indirect(cols(n2_l, lo, hi)), size2[t][:, lo:hi], ALU.add)
-            root = keep.tile([P, N], F32, name="root%d" % t)
-            nc.scalar.activation(root[:], den[t][:], ACT.Abs_reciprocal_sqrt, bias=0.5)
-            nc.scalar.activation(inv[t][:], root[:], ACT.Square, scale=0.25)
+
+        def invert(t, lo, hi, inv_tile):
+            root = keep.tile([P, hi - lo], F32, name="root%d_%d" % (t, lo))
+            nc.scalar.activation(root[:], den[t][:, lo:hi], ACT.Abs_reciprocal_sqrt, bias=0.5)
+            nc.scalar.activation(inv_tile[:], root[:], ACT.Square, scale=0.25)
+            for c, (a, b) in enumerate(Z_CHUNKS):
+                if lo <= a and b <= hi:
+                    inv[(t, c)] = inv_tile[:, a - lo : b - lo]
+
+        z_f = {}
 
         def quotient(t, c):
             lo, hi = Z_CHUNKS[c]
-            nc.vector.tensor_tensor(z_f[c][:, t, :], num[t][:].indirect(cols(n1_l, lo, hi)), inv[t][:, lo:hi], ALU.mult)
+            nc.vector.tensor_tensor(z_f[c][:, t, :], num[t][:].indirect(cols(n1_l, lo, hi)), inv[(t, c)], ALU.mult)
 
         score = [sb("score%d" % t, [P, N], F32) for t in range(PACK)]
-        z_b = [sb("z_b%d" % c, [P, hi - lo, PACK], BF16) for c, (lo, hi) in enumerate(Z_CHUNKS)]
-        s_ps = {}
+        z_b = {}
 
         def multiply(c):
             lo, hi = Z_CHUNKS[c]
@@ -151,32 +166,40 @@ def tile_picked_pqcnorm2gap_none_po_kernel(tc, x_words, x_scales, d_words, d_sca
             z_w = sb("z_w%d" % c, [P, w], U32)
             z_s = sb("z_s%d" % c, [P, w], U8)
             nc.vector.quantize_mx(out=z_w[:].bitcast(FP8X4), scales=z_s[:], in_=z_b[c][:].rearrange("p n t -> p (n t)"))
-            half = lo // 256
             for t in range(PACK):
-                if (half, t) not in s_ps:
-                    s_ps[(half, t)] = psum.tile([P, N], F32, name="bank%d" % ((PACK * (half + 1) + t) % 8))
-                bank = s_ps[(half, t)]
+                bank = psum.tile([P, N], F32, name="bank%d" % ((PACK * (c + 1) + t) % 8))
                 m = slice(t * P, (t + 1) * P)
-                nc.tensor.matmul_mx(bank[:, lo % 256 : lo % 256 + w], lhsT=xc_w[:, m].bitcast(FP8X4), lhsT_scale=xc_s[:, m],
+                nc.tensor.matmul_mx(bank[:, :w], lhsT=xc_w[:, m].bitcast(FP8X4), lhsT_scale=xc_s[:, m],
                                     rhs=z_w[:].bitcast(FP8X4), rhs_scale=z_s[:], start=True, stop=True)
-                if hi % 256 == 0:
-                    nc.scalar.activation(score[t][:, hi - 256 : hi], bank[:, :256], ACT.Copy, scale=0.0625)
+                nc.scalar.activation(score[t][:, lo:hi], bank[:, :w], ACT.Copy, scale=0.0625)
 
-        denominator(0)
-        denominator(1)
-        quotient(0, 0)
-        denominator(2)
-        denominator(3)
-        for t in range(1, PACK):
+        order = (2, 0, 1, 3)
+        numerator(order[0])
+        for t in order:
+            denominator(t)
+        for t in order[:3]:
+            invert(t, 0, N, sb("inv%d" % t, [P, N], F32))
+            if t != order[0]:
+                numerator(t)
+        numerator(3)
+        invert(3, 0, 256, stage.tile([P, 256], F32, name="inv3a", align_bytes=64, offset=12288))
+        invert(3, 256, N, sb("inv3b", [P, 256], F32))
+        z_f[0] = stage.tile([P, PACK, 256], F32, name="z_f0", align_bytes=64, offset=4096)
+        for t in order:
             quotient(t, 0)
+        z_b[0] = stage.tile([P, 256, PACK], BF16, name="z_b0", align_bytes=64, offset=8192)
         weave(nc.scalar.copy, z_b[0][:], z_f[0][:])
-        for t in range(PACK):
+        z_f[1] = stage.tile([P, PACK, 128], F32, name="z_f1", align_bytes=64, offset=12288)
+        for t in order:
             quotient(t, 1)
+        z_b[1] = sb("z_b1", [P, 128, PACK], BF16)
         weave(nc.scalar.copy, z_b[1][:], z_f[1][:])
         multiply(0)
-        for t in range(PACK):
+        z_f[2] = stage.tile([P, PACK, 128], F32, name="z_f2", align_bytes=64, offset=8192)
+        for t in order:
             quotient(t, 2)
         multiply(1)
+        z_b[2] = sb("z_b2", [P, 128, PACK], BF16)
         weave(nc.vector.tensor_copy, z_b[2][:], z_f[2][:])
         multiply(2)
 

@@ -21,8 +21,8 @@ PER_COL = 16
 FLOPS = 2 * 2 * 512 * 512 * 512
 
 HALVES = [(0, 256), (256, 512)]
-Z_CHUNKS = [(0, 256), (256, 384), (384, 512)]
-OUT_CHUNKS = [(0, 256), (256, 384), (384, 512)]
+Z_CHUNKS = HALVES
+OUT_CHUNKS = [(0, 256), (256, 512)]
 
 
 def cols(lst, lo, hi):
@@ -103,13 +103,13 @@ def tile_picked_pqcnorm2gap_none_po_kernel(tc, x_words, x_scales, d_words, d_sca
         dw_dealt = deal("dw_dealt", gather("dw_got", dw, k1_l, U32, 0), U32)
         xq_w = gather("xq_w", xw, offs_l, U32)
 
-        h_ps = []
-        for t in range(PACK):
+        h_ps = {}
+        for t in (1, 0, 2, 3):
             bank = psum.tile([P, N], F32, name="bank%d" % t)
             m = slice(t * P, (t + 1) * P)
             nc.tensor.matmul_mx(bank[:], lhsT=dw_dealt[:, m].bitcast(FP8X4), lhsT_scale=d_plane[:, m],
                                 rhs=xq_w[:].bitcast(FP8X4), rhs_scale=xq_s[:], start=True, stop=True)
-            h_ps.append(bank)
+            h_ps[t] = bank
 
         xc_w_got = gather("xc_w_got", xw, cand_l, U32, N)
         xc_s_got = gather("xc_s_got", xs, cand_l, U8, 0)
@@ -117,39 +117,37 @@ def tile_picked_pqcnorm2gap_none_po_kernel(tc, x_words, x_scales, d_words, d_sca
         xc_s = deal("xc_s", xc_s_got, U8)
 
 
-        size, size2, num, den = [], [], [], []
-        for t in range(PACK):
-            size.append(sb("size%d" % t, [P, N], F32))
-            if t == 3:
-                size2.append(stage.tile([P, N], F32, name="size2_3", align_bytes=64, offset=4096))
-            else:
-                size2.append(sb("size2_%d" % t, [P, N], F32))
-            num.append(sb("num%d" % t, [P, N], F32))
-            den.append(sb("den%d" % t, [P, N], F32))
+        size = [sb("size%d" % t, [P, N if t == 0 else 2 * N], F32) for t in range(PACK)]
+        size2 = [sb("size2_%d" % t, [P, N], F32) for t in range(PACK)]
+        num = [sb("num%d" % t, [P, N], F32) for t in range(PACK)]
+        den_last = sb("den_last", [P, N], F32)
+        den = [size[t + 1][:, N:] for t in range(PACK - 1)] + [den_last[:]]
+        score = [sb("score%d" % t, [P, 2 * N], F32) for t in range(PACK)]
 
-        for t in range(PACK):
-            nc.scalar.activation(size[t][:], h_ps[t][:], ACT.Abs, scale=0.0625)
-            if t == 2:
+        for t in (1, 0, 2, 3):
+            nc.scalar.activation(size[t][:, :N], h_ps[t][:], ACT.Abs, scale=0.0625)
+            if t == 0:
                 nc.scalar.activation(size2[t][:], h_ps[t][:], ACT.Abs, scale=0.0625)
             else:
-                nc.sync.dma_start(size2[t][:], size[t][:])
+                nc.sync.dma_start(size2[t][:], size[t][:, :N])
+        for t in range(PACK):
+            for lo, hi in HALVES if t == 0 else [(0, N)]:
+                nc.vector.tensor_tensor(den[t][:, lo:hi], size[t][:].indirect(cols(n2_l, lo, hi)), size2[t][:, lo:hi], ALU.add)
 
         inv = {}
 
         def numerator(t):
             nc.scalar.activation(num[t][:], h_ps[t][:], ACT.Copy, scale=gain[:, t : t + 1])
 
-        def denominator(t):
-            for lo, hi in HALVES:
-                nc.vector.tensor_tensor(den[t][:, lo:hi], size[t][:].indirect(cols(n2_l, lo, hi)), size2[t][:, lo:hi], ALU.add)
+        def root_of(t, lo, hi, root):
+            nc.scalar.activation(root, den[t][:, lo:hi], ACT.Abs_reciprocal_sqrt, bias=0.5)
 
-        def invert(t, lo, hi, inv_tile):
-            root = keep.tile([P, hi - lo], F32, name="root%d_%d" % (t, lo))
-            nc.scalar.activation(root[:], den[t][:, lo:hi], ACT.Abs_reciprocal_sqrt, bias=0.5)
-            nc.scalar.activation(inv_tile[:], root[:], ACT.Square, scale=0.25)
+        def square(t, lo, hi, root):
+            nc.scalar.activation(score[t][:, N + lo : N + hi], root[:], ACT.Square, scale=0.25)
+
+        for t in range(PACK):
             for c, (a, b) in enumerate(Z_CHUNKS):
-                if lo <= a and b <= hi:
-                    inv[(t, c)] = inv_tile[:, a - lo : b - lo]
+                inv[(t, c)] = score[t][:, N + a : N + b]
 
         z_f = {}
 
@@ -157,51 +155,63 @@ def tile_picked_pqcnorm2gap_none_po_kernel(tc, x_words, x_scales, d_words, d_sca
             lo, hi = Z_CHUNKS[c]
             nc.vector.tensor_tensor(z_f[c][:, t, :], num[t][:].indirect(cols(n1_l, lo, hi)), inv[(t, c)], ALU.mult)
 
-        score = [sb("score%d" % t, [P, N], F32) for t in range(PACK)]
         z_b = {}
 
-        def multiply(c):
-            lo, hi = Z_CHUNKS[c]
-            w = hi - lo
-            z_w = sb("z_w%d" % c, [P, w], U32)
-            z_s = sb("z_s%d" % c, [P, w], U8)
-            nc.vector.quantize_mx(out=z_w[:].bitcast(FP8X4), scales=z_s[:], in_=z_b[c][:].rearrange("p n t -> p (n t)"))
-            for t in range(PACK):
-                bank = psum.tile([P, N], F32, name="bank%d" % ((PACK * (c + 1) + t) % 8))
-                m = slice(t * P, (t + 1) * P)
-                nc.tensor.matmul_mx(bank[:, :w], lhsT=xc_w[:, m].bitcast(FP8X4), lhsT_scale=xc_s[:, m],
-                                    rhs=z_w[:].bitcast(FP8X4), rhs_scale=z_s[:], start=True, stop=True)
-                nc.scalar.activation(score[t][:, lo:hi], bank[:, :w], ACT.Copy, scale=0.0625)
+        z_w, z_s = {}, {}
 
-        order = (2, 0, 1, 3)
-        numerator(order[0])
-        for t in order:
-            denominator(t)
-        for t in order[:3]:
-            invert(t, 0, N, sb("inv%d" % t, [P, N], F32))
-            if t != order[0]:
-                numerator(t)
+        def quantise(c):
+            z_w[c] = sb("z_w%d" % c, [P, 256], U32)
+            z_s[c] = sb("z_s%d" % c, [P, 256], U8)
+            nc.vector.quantize_mx(out=z_w[c][:].bitcast(FP8X4), scales=z_s[c][:], in_=z_b[c][:].rearrange("p n t -> p (n t)"))
+
+        def multiply(t, c):
+            lo, hi = Z_CHUNKS[c]
+            bank = psum.tile([P, N], F32, name="bank%d" % ((PACK * (c + 1) + t) % 8))
+            m = slice(t * P, (t + 1) * P)
+            nc.tensor.matmul_mx(bank[:, :256], lhsT=xc_w[:, m].bitcast(FP8X4), lhsT_scale=xc_s[:, m],
+                                rhs=z_w[c][:].bitcast(FP8X4), rhs_scale=z_s[c][:], start=True, stop=True)
+            if (t, c) == (0, 1):
+                nc.vector.tensor_scalar(score[t][:, lo:hi], bank[:, :256], 0.0625, None, ALU.mult)
+            else:
+                nc.scalar.activation(score[t][:, lo:hi], bank[:, :256], ACT.Copy, scale=0.0625)
+
+        order = range(PACK)
+        roots = [sb("root%d" % t, [P, N], F32) for t in range(PACK - 1)]
+        root_a = stage.tile([P, 256], F32, name="root_a", align_bytes=64, offset=12288)
+        root_b = score[3][:, N + 256 :]
+        numerator(0)
+        numerator(1)
+        root_of(0, 0, N, roots[0][:])
+        numerator(2)
+        square(0, 0, N, roots[0])
+        root_of(1, 0, N, roots[1][:])
+        root_of(2, 0, N, roots[2][:])
+        square(1, 0, N, roots[1])
+        square(2, 0, N, roots[2])
+        root_of(3, 0, 256, root_a[:])
         numerator(3)
-        invert(3, 0, 256, stage.tile([P, 256], F32, name="inv3a", align_bytes=64, offset=12288))
-        invert(3, 256, N, sb("inv3b", [P, 256], F32))
+        square(3, 0, 256, root_a)
+        root_of(3, 256, N, root_b)
         z_f[0] = stage.tile([P, PACK, 256], F32, name="z_f0", align_bytes=64, offset=4096)
         for t in order:
             quotient(t, 0)
-        z_b[0] = stage.tile([P, 256, PACK], BF16, name="z_b0", align_bytes=64, offset=8192)
+        z_b[0] = sb("z_b0", [P, 256, PACK], BF16)
         weave(nc.scalar.copy, z_b[0][:], z_f[0][:])
-        z_f[1] = stage.tile([P, PACK, 128], F32, name="z_f1", align_bytes=64, offset=12288)
-        for t in order:
+        inv_b = stage.tile([P, 256], F32, name="inv_b", align_bytes=64, offset=4096)
+        nc.scalar.activation(inv_b[:], root_b, ACT.Square, scale=0.25)
+        inv[(3, 1)] = inv_b[:]
+        z_f[1] = stage.tile([P, PACK, 256], F32, name="z_f1", align_bytes=64, offset=12288)
+        for t in range(PACK - 1):
             quotient(t, 1)
-        z_b[1] = sb("z_b1", [P, 128, PACK], BF16)
-        weave(nc.scalar.copy, z_b[1][:], z_f[1][:])
-        multiply(0)
-        z_f[2] = stage.tile([P, PACK, 128], F32, name="z_f2", align_bytes=64, offset=8192)
-        for t in order:
-            quotient(t, 2)
-        multiply(1)
-        z_b[2] = sb("z_b2", [P, 128, PACK], BF16)
-        weave(nc.vector.tensor_copy, z_b[2][:], z_f[2][:])
-        multiply(2)
+        quantise(0)
+        quotient(3, 1)
+        z_b[1] = sb("z_b1", [P, 256, PACK], BF16)
+        weave(nc.vector.tensor_copy, z_b[1][:, :176, :], z_f[1][:, :, :176])
+        weave(nc.scalar.copy, z_b[1][:, 176:, :], z_f[1][:, :, 176:])
+        quantise(1)
+        for t in range(PACK):
+            for c in range(2):
+                multiply(t, c)
 
         out_rows = out_0.rearrange("(p t) j -> p t j", t=PACK)
         out_words = out_1[0].rearrange("p n t -> p (n t)").bitcast(I32)
@@ -212,14 +222,18 @@ def tile_picked_pqcnorm2gap_none_po_kernel(tc, x_words, x_scales, d_words, d_sca
             last = c == len(OUT_CHUNKS) - 1
             o_f = sb("o_f%d" % c, [P, PACK, w], F32)
             for pair in (0, 2):
-                if lo % 256 == 0:
+                if c == 0:
                     for t in (pair, pair + 1):
-                        nc.vector.tensor_copy(minus[t][:, lo : lo + 256], score[t][:].indirect(cols(n4_l, lo, lo + 256)))
+                        nc.vector.tensor_copy(minus[t][:], score[t][:].indirect(n4_l[:]))
                 for t in (pair, pair + 1):
                     nc.vector.tensor_tensor(o_f[:, t, :], score[t][:].indirect(cols(n3_l, lo, hi)), minus[t][:, lo:hi], ALU.subtract)
-            nc.sync.dma_start(out_rows[:, :, lo:hi], o_f[:])
+                nc.sync.dma_start(out_rows[:, pair : pair + 2, lo:hi], o_f[:, pair : pair + 2, :])
             o_b = sb("o_b%d" % c, [P, w, PACK], BF16)
-            weave(nc.vector.tensor_copy if last else nc.scalar.copy, o_b[:], o_f[:])
+            if last:
+                weave(nc.vector.tensor_copy, o_b[:, :176, :], o_f[:, :, :176])
+                weave(nc.scalar.copy, o_b[:, 176:, :], o_f[:, :, 176:])
+            else:
+                weave(nc.scalar.copy, o_b[:], o_f[:])
             o_w = sb("o_w%d" % c, [P, w], U32)
             nc.vector.quantize_mx(out=o_w[:].bitcast(FP8X4), scales=o_s[:, lo:hi], in_=o_b[:].rearrange("p n t -> p (n t)"))
             nc.sync.dma_start(out_words[:, lo:hi], o_w[:].bitcast(I32))

from contextlib import ExitStack

import concourse.mybir as mybir

F32 = mybir.dt.float32
BF16 = mybir.dt.bfloat16
I32 = mybir.dt.int32
U32 = mybir.dt.uint32
U16 = mybir.dt.uint16
U8 = mybir.dt.uint8
FP8X4 = mybir.dt.float8_e4m3fn_x4
ACT = mybir.ActivationFunctionType
ALU = mybir.AluOpType

P = 128
PACK = 4
N = 512
T = 1024
G = 2048
PER_COL = 16
FLOPS = 2 * 2 * 512 * 512 * 512

HALVES = [(0, 256), (256, 512)]
Z_CHUNKS = HALVES
OUT_CHUNKS = [(0, 256), (256, 512)]


def cols(lst, lo, hi):
    return lst[:, lo // PER_COL : hi // PER_COL]


def weave(engine_copy, dst, src):
    engine_copy(
        out=dst.rearrange("p (c i) t -> p c t i", i=4),
        in_=src.rearrange("p t (c i) -> p c t i", i=4),
    )


def tile_picked_pqcnorm2gap_none_po_kernel(tc, x_words, x_scales, d_words, d_scales, gs, offs, k1, n1, n2, cand, n3, n4, out_0, out_1, out_2):
    nc = tc.nc
    with ExitStack() as ctx:
        keep = ctx.enter_context(tc.tile_pool(name="keep", bufs=1))
        stage = ctx.enter_context(tc.tile_pool(name="stage", bufs=1))
        psum = ctx.enter_context(tc.psum_pool(name="psum", bufs=1))

        def sb(name, shape, dtype):
            return keep.tile(shape, dtype, name=name, align_bytes=64)

        def load_list(name, src):
            lst = keep.tile([P, N // PER_COL], U16, name=name)
            nc.sync.dma_start(lst[:], src)
            return lst

        warm = sb("warm", [P, 1], F32)
        warm_out = sb("warm_out", [P, 1], F32)
        nc.vector.memset(warm[:], 1.0)
        nc.scalar.activation(warm_out[:], warm[:], ACT.Abs_reciprocal_sqrt)

        xs = sb("xs", [P, T], U8)
        d_plane = sb("d_plane", [P, N], U8)
        nc.vector.memset(d_plane[:].bitcast(I32), 0)

        ds = sb("ds", [P, G], U8)
        nc.sync.dma_start(ds[:].bitcast(I32), d_scales[0].bitcast(I32).unsqueeze(1).to_broadcast([16, 8, G // 4]))
        k1_l = load_list("k1_l", k1)
        offs_l = load_list("offs_l", offs)
        for q in range(4):
            nc.sync.dma_start(xs[32 * q : 32 * q + 32, :].bitcast(I32), x_scales[0, 4 * q : 4 * q + 4, :].bitcast(I32).unsqueeze(0).to_broadcast([8, 4, T // 4]))
        dw = sb("dw", [P, G], U32)
        nc.sync.dma_start(dw[:].bitcast(I32), d_words[0].rearrange("p n t -> p (n t)").bitcast(I32))
        n2_l = load_list("n2_l", n2)
        gain = sb("gain", [P, PACK], F32)
        nc.sync.dma_start(gain[:], gs.rearrange("(p t) o -> p (t o)", t=PACK))
        n1_l = load_list("n1_l", n1)
        xw = sb("xw", [P, T], U32)
        nc.sync.dma_start(xw[:].bitcast(I32), x_words[0].rearrange("p n t -> p (n t)").bitcast(I32))

        def gather(name, table, lst, dtype, offset=None):
            if offset is None:
                got = sb(name, [P, N], dtype)
            else:
                got = stage.tile([P, N], dtype, name=name, align_bytes=64, offset=offset)
            nc.vector.tensor_copy(got[:], table[:].indirect(lst[:]))
            return got

        def deal(name, got, dtype):
            dealt = sb(name, [P, N], dtype)
            line = 4 if dtype == U32 else 16
            nc.vector.tensor_copy(
                dealt[:].rearrange("p (t c i) -> p c t i", t=PACK, i=line),
                got[:].rearrange("p (c i t) -> p c t i", t=PACK, i=line),
            )
            return dealt

        ds_dealt = deal("ds_dealt", gather("ds_got", ds, k1_l, U8), U8)
        for i in range(4):
            queue = nc.sync if i % 2 == 0 else nc.scalar
            queue.dma_start(d_plane[i:P:32, :].bitcast(I32), ds_dealt[8 * i : P : 32, :].bitcast(I32))
        cand_l = load_list("cand_l", cand)
        n4_l = load_list("n4_l", n4)
        n3_l = load_list("n3_l", n3)
        xq_s = gather("xq_s", xs, offs_l, U8)
        dw_dealt = deal("dw_dealt", gather("dw_got", dw, k1_l, U32, 0), U32)
        xq_w = gather("xq_w", xw, offs_l, U32)

        h_ps = {}
        for t in (1, 0, 2, 3):
            bank = psum.tile([P, N], F32, name="bank%d" % t)
            m = slice(t * P, (t + 1) * P)
            nc.tensor.matmul_mx(bank[:], lhsT=dw_dealt[:, m].bitcast(FP8X4), lhsT_scale=d_plane[:, m],
                                rhs=xq_w[:].bitcast(FP8X4), rhs_scale=xq_s[:], start=True, stop=True)
            h_ps[t] = bank

        xc_w_got = gather("xc_w_got", xw, cand_l, U32, N)
        xc_s_got = gather("xc_s_got", xs, cand_l, U8, 0)
        xc_w = deal("xc_w", xc_w_got, U32)
        xc_s = deal("xc_s", xc_s_got, U8)


        size = [sb("size%d" % t, [P, N if t == 0 else 2 * N], F32) for t in range(PACK)]
        size2 = [sb("size2_%d" % t, [P, N], F32) for t in range(PACK)]
        num = [sb("num%d" % t, [P, N], F32) for t in range(PACK)]
        den_last = sb("den_last", [P, N], F32)
        den = [size[t + 1][:, N:] for t in range(PACK - 1)] + [den_last[:]]
        score = [sb("score%d" % t, [P, 2 * N], F32) for t in range(PACK)]

        for t in (1, 0, 2, 3):
            nc.scalar.activation(size[t][:, :N], h_ps[t][:], ACT.Abs, scale=0.0625)
            if t == 0:
                nc.scalar.activation(size2[t][:], h_ps[t][:], ACT.Abs, scale=0.0625)
            else:
                nc.sync.dma_start(size2[t][:], size[t][:, :N])
        for t in range(PACK):
            for lo, hi in HALVES if t == 0 else [(0, N)]:
                nc.vector.tensor_tensor(den[t][:, lo:hi], size[t][:].indirect(cols(n2_l, lo, hi)), size2[t][:, lo:hi], ALU.add)

        inv = {}

        def numerator(t):
            nc.scalar.activation(num[t][:], h_ps[t][:], ACT.Copy, scale=gain[:, t : t + 1])

        def root_of(t, lo, hi, root):
            nc.scalar.activation(root, den[t][:, lo:hi], ACT.Abs_reciprocal_sqrt, bias=0.5)

        def square(t, lo, hi, root):
            nc.scalar.activation(score[t][:, N + lo : N + hi], root[:], ACT.Square, scale=0.25)

        for t in range(PACK):
            for c, (a, b) in enumerate(Z_CHUNKS):
                inv[(t, c)] = score[t][:, N + a : N + b]

        z_f = {}

        def quotient(t, c):
            lo, hi = Z_CHUNKS[c]
            nc.vector.tensor_tensor(z_f[c][:, t, :], num[t][:].indirect(cols(n1_l, lo, hi)), inv[(t, c)], ALU.mult)

        z_b = {}

        z_w, z_s = {}, {}

        def quantise(c):
            z_w[c] = sb("z_w%d" % c, [P, 256], U32)
            z_s[c] = sb("z_s%d" % c, [P, 256], U8)
            nc.vector.quantize_mx(out=z_w[c][:].bitcast(FP8X4), scales=z_s[c][:], in_=z_b[c][:].rearrange("p n t -> p (n t)"))

        def multiply(t, c):
            lo, hi = Z_CHUNKS[c]
            bank = psum.tile([P, N], F32, name="bank%d" % ((PACK * (c + 1) + t) % 8))
            m = slice(t * P, (t + 1) * P)
            nc.tensor.matmul_mx(bank[:, :256], lhsT=xc_w[:, m].bitcast(FP8X4), lhsT_scale=xc_s[:, m],
                                rhs=z_w[c][:].bitcast(FP8X4), rhs_scale=z_s[c][:], start=True, stop=True)
            if (t, c) == (0, 1):
                nc.vector.tensor_scalar(score[t][:, lo:hi], bank[:, :256], 0.0625, None, ALU.mult)
            else:
                nc.scalar.activation(score[t][:, lo:hi], bank[:, :256], ACT.Copy, scale=0.0625)

        order = range(PACK)
        roots = [sb("root%d" % t, [P, N], F32) for t in range(PACK - 1)]
        root_a = stage.tile([P, 256], F32, name="root_a", align_bytes=64, offset=12288)
        root_b = score[3][:, N + 256 :]
        numerator(0)
        numerator(1)
        root_of(0, 0, N, roots[0][:])
        numerator(2)
        square(0, 0, N, roots[0])
        root_of(1, 0, N, roots[1][:])
        root_of(2, 0, N, roots[2][:])
        square(1, 0, N, roots[1])
        square(2, 0, N, roots[2])
        root_of(3, 0, 256, root_a[:])
        numerator(3)
        square(3, 0, 256, root_a)
        root_of(3, 256, N, root_b)
        z_f[0] = stage.tile([P, PACK, 256], F32, name="z_f0", align_bytes=64, offset=4096)
        for t in order:
            quotient(t, 0)
        z_b[0] = sb("z_b0", [P, 256, PACK], BF16)
        weave(nc.scalar.copy, z_b[0][:], z_f[0][:])
        inv_b = stage.tile([P, 256], F32, name="inv_b", align_bytes=64, offset=4096)
        nc.scalar.activation(inv_b[:], root_b, ACT.Square, scale=0.25)
        inv[(3, 1)] = inv_b[:]
        z_f[1] = stage.tile([P, PACK, 256], F32, name="z_f1", align_bytes=64, offset=12288)
        for t in range(PACK - 1):
            quotient(t, 1)
        quantise(0)
        quotient(3, 1)
        z_b[1] = sb("z_b1", [P, 256, PACK], BF16)
        weave(nc.vector.tensor_copy, z_b[1][:, :176, :], z_f[1][:, :, :176])
        weave(nc.scalar.copy, z_b[1][:, 176:, :], z_f[1][:, :, 176:])
        quantise(1)
        for t in range(PACK):
            for c in range(2):
                multiply(t, c)

        out_rows = out_0.rearrange("(p t) j -> p t j", t=PACK)
        out_words = out_1[0].rearrange("p n t -> p (n t)").bitcast(I32)
        o_s = sb("o_s", [P, N], U8)
        minus = [sb("minus%d" % t, [P, N], F32) for t in range(PACK)]
        for c, (lo, hi) in enumerate(OUT_CHUNKS):
            w = hi - lo
            last = c == len(OUT_CHUNKS) - 1
            o_f = sb("o_f%d" % c, [P, PACK, w], F32)
            for pair in (0, 2):
                if c == 0:
                    for t in (pair, pair + 1):
                        nc.vector.tensor_copy(minus[t][:], score[t][:].indirect(n4_l[:]))
                for t in (pair, pair + 1):
                    nc.vector.tensor_tensor(o_f[:, t, :], score[t][:].indirect(cols(n3_l, lo, hi)), minus[t][:, lo:hi], ALU.subtract)
                nc.sync.dma_start(out_rows[:, pair : pair + 2, lo:hi], o_f[:, pair : pair + 2, :])
            o_b = sb("o_b%d" % c, [P, w, PACK], BF16)
            if last:
                weave(nc.vector.tensor_copy, o_b[:, :176, :], o_f[:, :, :176])
                weave(nc.scalar.copy, o_b[:, 176:, :], o_f[:, :, 176:])
            else:
                weave(nc.scalar.copy, o_b[:], o_f[:])
            o_w = sb("o_w%d" % c, [P, w], U32)
            nc.vector.quantize_mx(out=o_w[:].bitcast(FP8X4), scales=o_s[:, lo:hi], in_=o_b[:].rearrange("p n t -> p (n t)"))
            nc.sync.dma_start(out_words[:, lo:hi], o_w[:].bitcast(I32))
        for q in range(4):
            queue = nc.scalar if q % 4 != 3 else nc.sync
            queue.dma_start(out_2[0, 4 * q : 4 * q + 4, :].bitcast(I32), o_s[32 * q : 32 * q + 4, :].bitcast(I32))
